import numpy as np
import ml_dtypes


def mxq(x, axis, fmt="e4m3"):
    dtype, down = {"e4m3": (ml_dtypes.float8_e4m3fn, 7), "e5m2": (ml_dtypes.float8_e5m2, 14)}[fmt]
    v = np.moveaxis(np.asarray(x, np.float32).astype(ml_dtypes.bfloat16).astype(np.float64), axis, -1)
    blocks = v.reshape(v.shape[:-1] + (-1, 32))
    amax = np.abs(blocks).max(-1, keepdims=True)
    byte = np.maximum(np.where(amax > 0, np.frexp(amax)[1] - 1 + 127, 0) - down, 1)
    scale = np.exp2(byte - 127.0)
    codes = (blocks / scale).astype(np.float32).astype(dtype).astype(np.float64)
    return np.moveaxis((codes * scale).reshape(v.shape), -1, axis)


WIDE = False


def mx_kscale(k):
    if not WIDE:
        return np.ones(k)
    levels = np.array([10, -10, 5, -5, 0])
    if k % 512:
        return np.exp2(np.random.permutation(np.resize(levels, k // 32))).repeat(32)
    a = np.empty((k // 512, 16))
    for p in range(k // 512):
        a[p, :8] = np.random.permutation(np.resize(levels, 8))
        for g in range(8):
            far = levels[np.abs(levels - a[p, g]) >= 10]
            a[p, g + 8] = far[np.random.randint(len(far))]
    return np.exp2(a.ravel()).repeat(32)


def f64(x):
    return np.asarray(x).astype(np.float64)


def striped(idx):
    return np.tile(idx.reshape(-1, 16).T, (8, 1)).astype(np.uint16)


def unstriped(offs):
    return offs[:16].T.reshape(-1).astype(np.int64)


E2M1 = np.array([0.0, 0.5, 1.0, 1.5, 2.0, 3.0, 4.0, 6.0, -0.0, -0.5, -1.0, -1.5, -2.0, -3.0, -4.0, -6.0])


def pack_weight(w, fmt):
    k, n = w.shape
    w = f64(np.asarray(w, np.float32).astype(ml_dtypes.bfloat16)).reshape(k // 32, 32, n)
    amax = np.abs(w).max(1)
    if fmt == "e4m3":
        byte = np.frexp(amax)[1] - 1 + 127 - 7
    else:
        mant, ex = np.frexp(amax / 6.0)
        byte = np.where(mant > 0.5, ex, ex - 1) + 127
    byte = np.clip(np.where(amax > 0, byte, 1), 1, 254)
    scaled = (w * np.exp2(127.0 - byte)[:, None, :]).reshape(k, n).astype(np.float32)
    by_word = np.ascontiguousarray(scaled.reshape(k // 512, 128, 4, n).transpose(0, 1, 3, 2))
    if fmt == "e4m3":
        words = by_word.astype(ml_dtypes.float8_e4m3fn).view(np.uint8)
    else:
        c = by_word.astype(ml_dtypes.float4_e2m1fn).view(np.uint8) & 0xF
        words = (c[..., 0::2] | (c[..., 1::2] << 4)).reshape(k // 512, 128, 2 * n)
    return np.ascontiguousarray(words), np.ascontiguousarray(byte.astype(np.uint8).reshape(k // 512, 16, n))


def unpack_weight(words, scales, fmt):
    g, _, n = scales.shape
    words = np.ascontiguousarray(words).reshape(g, 128, n, -1)
    if fmt == "e4m3":
        vals = words.view(ml_dtypes.float8_e4m3fn).astype(np.float64)
    else:
        nib = np.empty((g, 128, n, 4), np.uint8)
        nib[..., 0::2] = words & 0xF
        nib[..., 1::2] = words >> 4
        vals = E2M1[nib]
    vals = vals * np.repeat(np.exp2(scales.astype(np.float64) - 127.0), 8, axis=1)[..., None]
    return vals.transpose(0, 1, 3, 2).reshape(g * 512, n)


def gelu(v):
    return 0.5 * v * (1.0 + np.tanh(np.sqrt(2.0 / np.pi) * (v + 0.044715 * v**3)))


K, H, N, T, S, P = 1024, 1024, 512, 2048, 1024, 512

def setup_inputs():
    n = np.random.standard_normal
    s = mx_kscale(K)[:, None]
    u = mx_kscale(H)[:, None]
    tab_words, tab_scales = pack_weight(n((K, T)) * s, "e4m3")
    w2_words, w2_scales = pack_weight(0.9 * n((K, H)) / np.sqrt(K) / s * u.T, "e2m1")
    return {
        "tab_words": tab_words, "tab_scales": tab_scales,
        "offs": striped(np.random.permutation(T)[:S]),
        "pos1": striped(np.random.permutation(S)[:P]),
        "pos2": striped(np.random.permutation(S)[:P]),
        "w1": (0.75 * n((K, H)) / np.sqrt(K) / s).astype(np.float32),
        "w2_words": w2_words, "w2_scales": w2_scales,
        "scl": np.random.uniform(0.4, 1.6, H).astype(np.float32),
        "expo": (0.5 * n(H)).astype(np.float32),
        "base": (P * np.random.uniform(0.5, 2.5, H)).astype(np.float32),
        "morph": (1.5 * P * n((H, P)) * u).astype(np.float32),
        "w3": (n((H, N)) / np.sqrt(H) / u).astype(np.float32),
    }

def reference(tab_words, tab_scales, offs, pos1, pos2, w1, w2_words, w2_scales, scl, expo, base, morph, w3):
    v = unpack_weight(tab_words, tab_scales, "e4m3")[:, unstriped(offs)]
    h = mxq(f64(w1), 0, "e4m3").T @ v
    g = unpack_weight(w2_words, w2_scales, "e2m1").T @ v
    a = np.exp(f64(scl)[:, None] * h[:, unstriped(pos1)] + f64(expo)[:, None])
    share = a / (f64(base)[:, None] + a.sum(axis=1)[:, None])
    x = share * f64(morph) + g[:, unstriped(pos2)]
    y = mxq(f64(w3), 0, "e4m3").T @ mxq(x, 0, "e4m3")
    return np.tanh(y)

@@ -1,0 +1,302 @@
+from contextlib import ExitStack
+
+import concourse.mybir as mybir
+
+K, H, N, T, S, M = 1024, 1024, 512, 2048, 1024, 512
+FLOPS = 2 * (2 * K * H * S + H * N * M)
+
+F32 = mybir.dt.float32
+BF16 = mybir.dt.bfloat16
+I32 = mybir.dt.int32
+U32 = mybir.dt.uint32
+U16 = mybir.dt.uint16
+U8 = mybir.dt.uint8
+FP8X4 = mybir.dt.float8_e4m3fn_x4
+FP4X4 = mybir.dt.float4_e2m1fn_x4
+ACT = mybir.ActivationFunctionType
+ALU = mybir.AluOpType
+
+P = 128
+PACK = 4
+PASS = P * PACK
+BANK = 512
+
+
+def tile_list_colony_confirmation_scores_kernel(
+    tc, tab_words, tab_scales, offs, pos1, pos2, w1, w2_words, w2_scales, scl, expo, base, morph, w3, out
+):
+    nc = tc.nc
+    k_passes = K // PASS
+    r_passes = H // PASS
+    halves = S // BANK
+
+    with ExitStack() as ctx:
+        keep = ctx.enter_context(tc.tile_pool(name="keep", bufs=1))
+        ring = ctx.enter_context(tc.tile_pool(name="ring", bufs=3))
+        acc = ctx.enter_context(tc.psum_pool(name="acc", bufs=4))
+        fin = ctx.enter_context(tc.psum_pool(name="fin", bufs=1))
+
+        def held(shape, dtype, name):
+            return keep.tile(shape, dtype, name=name, align_bytes=64)
+
+        def rounded():
+            return keep.tile([P, PASS * PACK], BF16, name="rounded", bufs=4, align_bytes=64)
+
+        offs_t = held([P, S // 16], U16, "offs_t")
+        pos1_t = held([P, M // 16], U16, "pos1_t")
+        pos2_t = held([P, M // 16], U16, "pos2_t")
+
+        tab_s = held([P, T], U8, "tab_s")
+        w2_s_raw = held([P, k_passes, H], U8, "w2_s_raw")
+        v_s1 = [held([P, BANK], U8, f"v_s1{hf}") for hf in range(halves)]
+        tab_s_words = tab_s[:].bitcast(I32)
+        nc.vector.memset(tab_s_words[:, : T // 8], 0)
+        nc.gpsimd.memset(tab_s_words[:, T // 8 :], 0)
+        nc.gpsimd.memset(w2_s_raw[:].bitcast(I32), 0)
+        for hf in range(halves):
+            nc.vector.memset(v_s1[hf][:].bitcast(I32), 0)
+
+        for q in range(4):
+            nc.scalar.dma_start(
+                out=tab_s[32 * q : 32 * q + 4 * k_passes, :].bitcast(I32),
+                in_=tab_scales[:, 4 * q : 4 * q + 4, :].bitcast(I32),
+            )
+        for q in range(4):
+            nc.gpsimd.dma_start(
+                out=w2_s_raw[32 * q : 32 * q + 4, :, :].bitcast(I32),
+                in_=w2_scales[:, 4 * q : 4 * q + 4, :].rearrange("a r c -> r a c").bitcast(I32),
+            )
+        nc.sync.dma_start(offs_t[:], offs)
+        nc.sync.dma_start(pos1_t[:], pos1)
+        nc.sync.dma_start(pos2_t[:], pos2)
+
+        tab_w = [held([P, T], I32, f"tab_w{a}") for a in range(k_passes)]
+        w2_w_raw = held([P, k_passes, H], U16, "w2_w_raw")
+        w1_raw = {(b, a): held([P, PACK, PASS], F32, f"w1_raw{b}{a}") for b in range(r_passes) for a in range(k_passes)}
+        morph_t = [held([P, PACK, M], F32, f"morph_t{b}") for b in range(r_passes)]
+        w3_raw = [held([P, PACK, N], F32, f"w3_raw{b}") for b in range(r_passes)]
+
+        def load_table(a):
+            nc.sync.dma_start(out=tab_w[a][:], in_=tab_words[a].rearrange("p t i -> p (t i)").bitcast(I32))
+
+        def load_w1(b):
+            for a in range(k_passes):
+                nc.sync.dma_start(
+                    out=w1_raw[b, a][:],
+                    in_=w1[PASS * a : PASS * (a + 1), PASS * b : PASS * (b + 1)].rearrange("(p j) c -> p j c", j=PACK),
+                )
+
+        def load_rows(tile, src, b):
+            nc.sync.dma_start(out=tile[:], in_=src[PASS * b : PASS * (b + 1), :].rearrange("(p i) c -> p i c", i=PACK))
+
+        load_table(0)
+        nc.sync.dma_start(out=w2_w_raw[:].bitcast(I32), in_=w2_words.rearrange("a p c -> p a c").bitcast(I32))
+        load_table(1)
+        load_w1(0)
+        rows = {}
+        for name, vec in (("scl", scl), ("expo", expo), ("base", base)):
+            rows[name] = held([P, r_passes * PACK], F32, name + "_t")
+            nc.sync.dma_start(
+                out=rows[name][:].rearrange("p (b i) -> p b i", i=PACK),
+                in_=vec.rearrange("(b p i) -> p b i", p=P, i=PACK),
+            )
+        load_rows(morph_t[0], morph, 0)
+        load_w1(1)
+        load_rows(morph_t[1], morph, 1)
+        load_rows(w3_raw[0], w3, 0)
+        load_rows(w3_raw[1], w3, 1)
+
+        v_s, v_w = {}, {}
+
+        def list_half(hf):
+            return offs_t[:, hf * BANK // 16 : (hf + 1) * BANK // 16]
+
+        def gather_scales(hf):
+            v_s[hf] = held([P, BANK], U8, f"v_s{hf}")
+            nc.vector.tensor_copy(out=v_s[hf][:], in_=tab_s[:].indirect(list_half(hf)))
+            nc.gpsimd.dma_start(out=v_s1[hf][0:100, :].bitcast(I32), in_=v_s[hf][4:104, :].bitcast(I32))
+
+        def gather_words(a, hf):
+            v_w[a, hf] = held([P, BANK], U32, f"v_w{a}{hf}")
+            nc.vector.tensor_copy(out=v_w[a, hf][:], in_=tab_w[a][:].bitcast(U32).indirect(list_half(hf)))
+
+        def deal_w2(raw, dtype, name):
+            dealt = held([P, k_passes * H], dtype, name)
+            nc.vector.tensor_copy(
+                out=dealt[:].rearrange("p (g t m) -> p g t m", t=PACK, m=P),
+                in_=raw[:].rearrange("p a (b m t) -> p (a b) t m", t=PACK, m=P),
+            )
+            return dealt
+
+        gather_scales(0)
+        w2_s = deal_w2(w2_s_raw, U8, "w2_s")
+        gather_words(0, 0)
+        w2_w = deal_w2(w2_w_raw, U16, "w2_w")
+        gather_words(1, 0)
+        gather_scales(1)
+        gather_words(0, 1)
+        gather_words(1, 1)
+
+        def quantise(grouped, name):
+            codes = held([P, PASS], U32, name + "_c")
+            scales = held([P, PASS], U8, name + "_s")
+            nc.vector.quantize_mx(out=codes[:].bitcast(FP8X4), scales=scales[:], in_=grouped[:])
+            return codes, scales
+
+        def round_on_gpsimd(dst, src):
+            nc.gpsimd.tensor_scalar(out=dst, in0=src, scalar1=1.0, scalar2=0.0, op0=ALU.mult, op1=ALU.add)
+
+        w1_q = {}
+
+        def prepare_w1(b):
+            for a in range(k_passes):
+                grouped = rounded()
+                dst = grouped[:].rearrange("p (t m j) -> p m t j", t=PACK, j=PACK)
+                src = w1_raw[b, a][:].rearrange("p j (m t) -> p m t j", t=PACK)
+                round_on_gpsimd(dst, src)
+                w1_q[b, a] = quantise(grouped, f"w1_q{b}{a}")
+
+        w3_q = {}
+
+        def prepare_w3(b):
+            grouped = rounded()
+            round_on_gpsimd(grouped[:].rearrange("p (n i) -> p n i", i=PACK), w3_raw[b][:].rearrange("p i n -> p n i"))
+            w3_q[b] = quantise(grouped, f"w3_q{b}")
+
+        def first_stage(dst, hf, lhs_of_pass, rhs_scale_of_pass):
+            bank = acc.tile([P, BANK], F32, name="bank")
+            for a in range(k_passes):
+                codes, scales = lhs_of_pass(a)
+                nc.tensor.matmul_mx(
+                    out=bank[:],
+                    lhsT=codes,
+                    lhsT_scale=scales,
+                    rhs=v_w[a, hf][:].bitcast(FP8X4),
+                    rhs_scale=rhs_scale_of_pass(a),
+                    start=(a == 0),
+                    stop=(a == k_passes - 1),
+                )
+            nc.scalar.copy(out=dst[:, hf * BANK : (hf + 1) * BANK], in_=bank[:])
+
+        g_t = {(b, i): held([P, S], F32, f"g{b}{i}") for b in range(r_passes) for i in range(PACK)}
+
+        def make_g(b, i, hf):
+            c0 = PASS * b + P * i
+
+            def lhs(a):
+                cols = slice(a * H + c0, a * H + c0 + P)
+                return w2_w[:, cols].bitcast(FP4X4), w2_s[:, cols]
+
+            first_stage(g_t[b, i], hf, lhs, lambda a: (v_s, v_s1)[a][hf][:])
+
+        denom = held([P, r_passes * PACK], F32, "denom")
+        inv = held([P, r_passes * PACK], F32, "inv")
+        x_f32 = [held([P, PACK, M], F32, f"x_f32{b}") for b in range(r_passes)]
+        a_t, share = {}, {}
+
+        def col(b, i):
+            return slice(PACK * b + i, PACK * b + i + 1)
+
+        def look(b, i):
+            h_t = ring.tile([P, S], F32, name="h_t")
+
+            def lhs(a):
+                codes, scales = w1_q[b, a]
+                cols = slice(P * i, P * (i + 1))
+                return codes[:, cols].bitcast(FP8X4), scales[:, cols]
+
+            for hf in range(halves):
+                first_stage(h_t, hf, lhs, lambda a: v_s[hf][4 * a :, :])
+            a_t[b, i] = ring.tile([P, M], F32, name="a_t")
+            nc.scalar.activation(
+                out=a_t[b, i][:],
+                in_=h_t[:].indirect(pos1_t[:]),
+                func=ACT.Exp,
+                bias=rows["expo"][:, col(b, i)],
+                scale=rows["scl"][:, col(b, i)],
+            )
+
+        def row_sum(b, i):
+            passed = ring.tile([P, M], BF16, name="passed")
+            nc.vector.tensor_scalar(
+                out=passed[:],
+                in0=a_t[b, i][:],
+                scalar1=1.0,
+                scalar2=rows["base"][:, col(b, i)],
+                op0=ALU.mult,
+                op1=ALU.add,
+                accum_out=denom[:, col(b, i)],
+            )
+
+        def invert(b, i):
+            nc.vector.reciprocal(out=inv[:, col(b, i)], in_=denom[:, col(b, i)])
+
+        def weigh(b, i):
+            share[b, i] = ring.tile([P, M], F32, name="share")
+            nc.vector.scalar_tensor_tensor(
+                out=share[b, i][:],
+                in0=a_t[b, i][:],
+                scalar=inv[:, col(b, i)],
+                in1=morph_t[b][:, i, :],
+                op0=ALU.mult,
+                op1=ALU.mult,
+            )
+
+        def add_picked(b, i):
+            nc.vector.tensor_tensor(
+                out=x_f32[b][:, i, :], in0=g_t[b, i][:].indirect(pos2_t[:]), in1=share[b, i][:], op=ALU.add
+            )
+
+        y = [fin.tile([P, M], F32, name=f"y{nt}") for nt in range(N // P)]
+
+        def second_stage(b):
+            grouped = rounded()
+            nc.vector.tensor_copy(
+                out=grouped[:].rearrange("p (c e i) -> p c i e", e=4, i=PACK),
+                in_=x_f32[b][:].rearrange("p i (c e) -> p c i e", e=4),
+            )
+            x_c, x_s = quantise(grouped, f"x_q{b}")
+            w_c, w_s = w3_q[b]
+            for nt in range(N // P):
+                cols = slice(P * nt, P * (nt + 1))
+                nc.tensor.matmul_mx(
+                    out=y[nt][:],
+                    lhsT=w_c[:, cols].bitcast(FP8X4),
+                    lhsT_scale=w_s[:, cols],
+                    rhs=x_c[:].bitcast(FP8X4),
+                    rhs_scale=x_s[:],
+                    start=(b == 0),
+                    stop=(b == r_passes - 1),
+                )
+
+        tiles = [(b, i) for b in range(r_passes) for i in range(PACK)]
+        for b, i in tiles:
+            make_g(b, i, 0)
+        prepare_w1(0)
+        for b, i in tiles:
+            make_g(b, i, 1)
+        for n, tile in enumerate(tiles + [None]):
+            before = tiles[n - 1] if n > 0 else None
+            if n == 2:
+                prepare_w1(1)
+            if n == 5:
+                prepare_w3(0)
+            if n == 7:
+                prepare_w3(1)
+            if tile:
+                look(*tile)
+                row_sum(*tile)
+            if before:
+                weigh(*before)
+            if tile:
+                invert(*tile)
+            if before:
+                add_picked(*before)
+            if n == 6:
+                second_stage(0)
+        second_stage(1)
+
+        for nt in range(N // P):
+            res = held([P, M], F32, f"res{nt}")
+            nc.scalar.activation(out=res[:], in_=y[nt][:], func=ACT.Tanh)
+            nc.sync.dma_start(out=out[P * nt : P * (nt + 1), :], in_=res[:])

@@ -20,6 +20,7 @@ P = 128
 PACK = 4
 PASS = P * PACK
 BANK = 512
+SUMS_ON_SCALAR = 3
 
 
 def tile_list_colony_confirmation_scores_kernel(
@@ -46,29 +47,25 @@ def tile_list_colony_confirmation_scores_kernel(
         pos1_t = held([P, M // 16], U16, "pos1_t")
         pos2_t = held([P, M // 16], U16, "pos2_t")
 
-        tab_s = held([P, T], U8, "tab_s")
+        tab_s = held([P, k_passes * T], U8, "tab_s")
         w2_s_raw = held([P, k_passes, H], U8, "w2_s_raw")
-        v_s1 = [held([P, BANK], U8, f"v_s1{hf}") for hf in range(halves)]
         tab_s_words = tab_s[:].bitcast(I32)
-        nc.vector.memset(tab_s_words[:, : T // 8], 0)
-        nc.gpsimd.memset(tab_s_words[:, T // 8 :], 0)
-        nc.gpsimd.memset(w2_s_raw[:].bitcast(I32), 0)
-        for hf in range(halves):
-            nc.vector.memset(v_s1[hf][:].bitcast(I32), 0)
+        nc.vector.memset(tab_s_words[:, : T // 4], 0)
+        nc.gpsimd.memset(tab_s_words[:, T // 4 :], 0)
+        w2_s_words = w2_s_raw[:].rearrange("p a c -> p (a c)").bitcast(I32)
+        nc.vector.memset(w2_s_words[:, : H // 4], 0)
+        nc.gpsimd.memset(w2_s_words[:, H // 4 :], 0)
 
-        for q in range(4):
-            nc.scalar.dma_start(
-                out=tab_s[32 * q : 32 * q + 4 * k_passes, :].bitcast(I32),
-                in_=tab_scales[:, 4 * q : 4 * q + 4, :].bitcast(I32),
-            )
-        for q in range(4):
-            nc.gpsimd.dma_start(
-                out=w2_s_raw[32 * q : 32 * q + 4, :, :].bitcast(I32),
-                in_=w2_scales[:, 4 * q : 4 * q + 4, :].rearrange("a r c -> r a c").bitcast(I32),
-            )
         nc.sync.dma_start(offs_t[:], offs)
         nc.sync.dma_start(pos1_t[:], pos1)
         nc.sync.dma_start(pos2_t[:], pos2)
+        rows = {}
+        for name, vec in (("scl", scl), ("expo", expo), ("base", base)):
+            rows[name] = held([P, r_passes * PACK], F32, name + "_t")
+            nc.sync.dma_start(
+                out=rows[name][:].rearrange("p (b i) -> p b i", i=PACK),
+                in_=vec.rearrange("(b p i) -> p b i", p=P, i=PACK),
+            )
 
         tab_w = [held([P, T], I32, f"tab_w{a}") for a in range(k_passes)]
         w2_w_raw = held([P, k_passes, H], U16, "w2_w_raw")
@@ -91,15 +88,18 @@ def tile_list_colony_confirmation_scores_kernel(
 
         load_table(0)
         nc.sync.dma_start(out=w2_w_raw[:].bitcast(I32), in_=w2_words.rearrange("a p c -> p a c").bitcast(I32))
-        load_table(1)
-        load_w1(0)
-        rows = {}
-        for name, vec in (("scl", scl), ("expo", expo), ("base", base)):
-            rows[name] = held([P, r_passes * PACK], F32, name + "_t")
+        for q in range(4):
             nc.sync.dma_start(
-                out=rows[name][:].rearrange("p (b i) -> p b i", i=PACK),
-                in_=vec.rearrange("(b p i) -> p b i", p=P, i=PACK),
+                out=tab_s_words[32 * q : 32 * q + 4, :].rearrange("r (a c) -> r a c", a=k_passes),
+                in_=tab_scales[:, 4 * q : 4 * q + 4, :].rearrange("a r c -> r a c").bitcast(I32),
             )
+        load_table(1)
+        for q in range(4):
+            nc.sync.dma_start(
+                out=w2_s_raw[32 * q : 32 * q + 4, :, :].bitcast(I32),
+                in_=w2_scales[:, 4 * q : 4 * q + 4, :].rearrange("a r c -> r a c").bitcast(I32),
+            )
+        load_w1(0)
         load_rows(morph_t[0], morph, 0)
         load_w1(1)
         load_rows(morph_t[1], morph, 1)
@@ -111,10 +111,9 @@ def tile_list_colony_confirmation_scores_kernel(
         def list_half(hf):
             return offs_t[:, hf * BANK // 16 : (hf + 1) * BANK // 16]
 
-        def gather_scales(hf):
-            v_s[hf] = held([P, BANK], U8, f"v_s{hf}")
-            nc.vector.tensor_copy(out=v_s[hf][:], in_=tab_s[:].indirect(list_half(hf)))
-            nc.gpsimd.dma_start(out=v_s1[hf][0:100, :].bitcast(I32), in_=v_s[hf][4:104, :].bitcast(I32))
+        def gather_scales(a, hf):
+            v_s[a, hf] = held([P, BANK], U8, f"v_s{a}{hf}")
+            nc.vector.tensor_copy(out=v_s[a, hf][:], in_=tab_s[:, a * T : (a + 1) * T].indirect(list_half(hf)))
 
         def gather_words(a, hf):
             v_w[a, hf] = held([P, BANK], U32, f"v_w{a}{hf}")
@@ -128,14 +127,15 @@ def tile_list_colony_confirmation_scores_kernel(
             )
             return dealt
 
-        gather_scales(0)
-        w2_s = deal_w2(w2_s_raw, U8, "w2_s")
         gather_words(0, 0)
         w2_w = deal_w2(w2_w_raw, U16, "w2_w")
+        gather_scales(0, 0)
+        gather_scales(1, 0)
         gather_words(1, 0)
-        gather_scales(1)
-        gather_words(0, 1)
-        gather_words(1, 1)
+        w2_s = deal_w2(w2_s_raw, U8, "w2_s")
+        for a in range(k_passes):
+            gather_words(a, 1)
+            gather_scales(a, 1)
 
         def quantise(grouped, name):
             codes = held([P, PASS], U32, name + "_c")
@@ -163,7 +163,7 @@ def tile_list_colony_confirmation_scores_kernel(
             round_on_gpsimd(grouped[:].rearrange("p (n i) -> p n i", i=PACK), w3_raw[b][:].rearrange("p i n -> p n i"))
             w3_q[b] = quantise(grouped, f"w3_q{b}")
 
-        def first_stage(dst, hf, lhs_of_pass, rhs_scale_of_pass):
+        def first_stage(dst, hf, lhs_of_pass, copy_out):
             bank = acc.tile([P, BANK], F32, name="bank")
             for a in range(k_passes):
                 codes, scales = lhs_of_pass(a)
@@ -172,22 +172,22 @@ def tile_list_colony_confirmation_scores_kernel(
                     lhsT=codes,
                     lhsT_scale=scales,
                     rhs=v_w[a, hf][:].bitcast(FP8X4),
-                    rhs_scale=rhs_scale_of_pass(a),
+                    rhs_scale=v_s[a, hf][:],
                     start=(a == 0),
                     stop=(a == k_passes - 1),
                 )
-            nc.scalar.copy(out=dst[:, hf * BANK : (hf + 1) * BANK], in_=bank[:])
+            copy_out(out=dst[:, hf * BANK : (hf + 1) * BANK], in_=bank[:])
 
         g_t = {(b, i): held([P, S], F32, f"g{b}{i}") for b in range(r_passes) for i in range(PACK)}
 
-        def make_g(b, i, hf):
+        def make_g(b, i, hf, copy_out):
             c0 = PASS * b + P * i
 
             def lhs(a):
                 cols = slice(a * H + c0, a * H + c0 + P)
                 return w2_w[:, cols].bitcast(FP4X4), w2_s[:, cols]
 
-            first_stage(g_t[b, i], hf, lhs, lambda a: (v_s, v_s1)[a][hf][:])
+            first_stage(g_t[b, i], hf, lhs, copy_out)
 
         denom = held([P, r_passes * PACK], F32, "denom")
         inv = held([P, r_passes * PACK], F32, "inv")
@@ -206,7 +206,7 @@ def tile_list_colony_confirmation_scores_kernel(
                 return codes[:, cols].bitcast(FP8X4), scales[:, cols]
 
             for hf in range(halves):
-                first_stage(h_t, hf, lhs, lambda a: v_s[hf][4 * a :, :])
+                first_stage(h_t, hf, lhs, nc.scalar.copy)
             a_t[b, i] = ring.tile([P, M], F32, name="a_t")
             nc.scalar.activation(
                 out=a_t[b, i][:],
@@ -214,6 +214,15 @@ def tile_list_colony_confirmation_scores_kernel(
                 func=ACT.Exp,
                 bias=rows["expo"][:, col(b, i)],
                 scale=rows["scl"][:, col(b, i)],
+            )
+
+        sums = held([P, r_passes * PACK], F32, "sums")
+
+        def row_sum_on_scalar(b, i):
+            passed = ring.tile([P, M], BF16, name="passed_s")
+            nc.scalar.activation(out=passed[:], in_=a_t[b, i][:], func=ACT.Copy, accum_out=sums[:, col(b, i)])
+            nc.scalar.activation(
+                out=denom[:, col(b, i)], in_=sums[:, col(b, i)], func=ACT.Identity, bias=rows["base"][:, col(b, i)]
             )
 
         def row_sum(b, i):
@@ -247,35 +256,56 @@ def tile_list_colony_confirmation_scores_kernel(
                 out=x_f32[b][:, i, :], in0=g_t[b, i][:].indirect(pos2_t[:]), in1=share[b, i][:], op=ALU.add
             )
 
-        y = [fin.tile([P, M], F32, name=f"y{nt}") for nt in range(N // P)]
+        HALF = M // 2
+        y = {(hm, pair): fin.tile([P, 2, HALF], F32, name=f"y{hm}{pair}") for hm in range(2) for pair in range(2)}
 
-        def second_stage(b):
+        def quantise_x(b, m0, width):
             grouped = rounded()
             nc.vector.tensor_copy(
-                out=grouped[:].rearrange("p (c e i) -> p c i e", e=4, i=PACK),
-                in_=x_f32[b][:].rearrange("p i (c e) -> p c i e", e=4),
+                out=grouped[:, : width * PACK].rearrange("p (c e i) -> p c i e", e=4, i=PACK),
+                in_=x_f32[b][:, :, m0 : m0 + width].rearrange("p i (c e) -> p c i e", e=4),
             )
-            x_c, x_s = quantise(grouped, f"x_q{b}")
+            codes = held([P, width], U32, f"x_c{b}{m0}")
+            scales = held([P, width], U8, f"x_s{b}{m0}")
+            nc.vector.quantize_mx(out=codes[:].bitcast(FP8X4), scales=scales[:], in_=grouped[:, : width * PACK])
+            return codes, scales
+
+        def second_stage(b, hm, x_c, x_s):
             w_c, w_s = w3_q[b]
-            for nt in range(N // P):
-                cols = slice(P * nt, P * (nt + 1))
-                nc.tensor.matmul_mx(
-                    out=y[nt][:],
-                    lhsT=w_c[:, cols].bitcast(FP8X4),
-                    lhsT_scale=w_s[:, cols],
-                    rhs=x_c[:].bitcast(FP8X4),
-                    rhs_scale=x_s[:],
-                    start=(b == 0),
-                    stop=(b == r_passes - 1),
+            for pair in range(2):
+                for u in range(2):
+                    cols = slice(P * (2 * pair + u), P * (2 * pair + u + 1))
+                    nc.tensor.matmul_mx(
+                        out=y[hm, pair][:, u, :],
+                        lhsT=w_c[:, cols].bitcast(FP8X4),
+                        lhsT_scale=w_s[:, cols],
+                        rhs=x_c.bitcast(FP8X4),
+                        rhs_scale=x_s,
+                        start=(b == 0 and u == 0),
+                        stop=(b == r_passes - 1 and u == 1),
+                    )
+
+        def finish(hm):
+            for pair in range(2):
+                res = held([P, 2, HALF], F32, f"res{hm}{pair}")
+                nc.scalar.activation(out=res[:], in_=y[hm, pair][:], func=ACT.Tanh)
+                nc.sync.dma_start(
+                    out=out[2 * P * pair : 2 * P * (pair + 1), hm * HALF : (hm + 1) * HALF].rearrange("(u p) m -> p u m", p=P),
+                    in_=res[:],
                 )
 
         tiles = [(b, i) for b in range(r_passes) for i in range(PACK)]
+        last = tiles[-1]
         for b, i in tiles:
-            make_g(b, i, 0)
+            make_g(b, i, 0, nc.scalar.copy)
         prepare_w1(0)
-        for b, i in tiles:
-            make_g(b, i, 1)
-        for n, tile in enumerate(tiles + [None]):
+        for i in range(PACK):
+            make_g(0, i, 1, nc.scalar.copy)
+        for i in range(PACK):
+            make_g(1, i, 1, nc.vector.tensor_copy)
+        picked_last = held([P, M], F32, "picked_last")
+        nc.vector.tensor_copy(out=picked_last[:], in_=g_t[last][:].indirect(pos2_t[:]))
+        for n, tile in enumerate(tiles):
             before = tiles[n - 1] if n > 0 else None
             if n == 2:
                 prepare_w1(1)
@@ -283,20 +313,36 @@ def tile_list_colony_confirmation_scores_kernel(
                 prepare_w3(0)
             if n == 7:
                 prepare_w3(1)
-            if tile:
-                look(*tile)
+            look(*tile)
+            if n < SUMS_ON_SCALAR:
+                row_sum_on_scalar(*tile)
+            else:
                 row_sum(*tile)
             if before:
                 weigh(*before)
-            if tile:
-                invert(*tile)
+            invert(*tile)
             if before:
                 add_picked(*before)
             if n == 6:
-                second_stage(0)
-        second_stage(1)
+                x_c, x_s = quantise_x(0, 0, M)
+                for hm in range(2):
+                    cols = slice(hm * HALF, (hm + 1) * HALF)
+                    second_stage(0, hm, x_c[:, cols], x_s[:, cols])
 
-        for nt in range(N // P):
-            res = held([P, M], F32, f"res{nt}")
-            nc.scalar.activation(out=res[:], in_=y[nt][:], func=ACT.Tanh)
-            nc.sync.dma_start(out=out[P * nt : P * (nt + 1), :], in_=res[:])
+        b, i = last
+        weighed_last = held([P, M], F32, "weighed_last")
+        nc.vector.tensor_tensor(out=weighed_last[:], in0=a_t[last][:], in1=morph_t[b][:, i, :], op=ALU.mult)
+        for hm in range(2):
+            cols = slice(hm * HALF, (hm + 1) * HALF)
+            nc.vector.scalar_tensor_tensor(
+                out=x_f32[b][:, i, cols],
+                in0=weighed_last[:, cols],
+                scalar=inv[:, col(b, i)],
+                in1=picked_last[:, cols],
+                op0=ALU.mult,
+                op1=ALU.add,
+            )
+        for hm in range(2):
+            x_c, x_s = quantise_x(b, hm * HALF, HALF)
+            second_stage(b, hm, x_c[:], x_s[:])
+            finish(hm)

@@ -20,7 +20,8 @@ P = 128
 PACK = 4
 PASS = P * PACK
 BANK = 512
-SUMS_ON_SCALAR = 3
+PART = 128
+SUMS_ON_VECTOR = 3
 
 
 def tile_list_colony_confirmation_scores_kernel(
@@ -33,12 +34,15 @@ def tile_list_colony_confirmation_scores_kernel(
 
     with ExitStack() as ctx:
         keep = ctx.enter_context(tc.tile_pool(name="keep", bufs=1))
+        shared = ctx.enter_context(tc.tile_pool(name="shared", bufs=1))
         ring = ctx.enter_context(tc.tile_pool(name="ring", bufs=3))
         acc = ctx.enter_context(tc.psum_pool(name="acc", bufs=4))
         fin = ctx.enter_context(tc.psum_pool(name="fin", bufs=1))
 
-        def held(shape, dtype, name):
-            return keep.tile(shape, dtype, name=name, align_bytes=64)
+        def held(shape, dtype, name, offset=None):
+            if offset is None:
+                return keep.tile(shape, dtype, name=name, align_bytes=64)
+            return shared.tile(shape, dtype, name=name, align_bytes=64, offset=offset)
 
         def rounded():
             return keep.tile([P, PASS * PACK], BF16, name="rounded", bufs=4, align_bytes=64)
@@ -48,24 +52,13 @@ def tile_list_colony_confirmation_scores_kernel(
         pos2_t = held([P, M // 16], U16, "pos2_t")
 
         tab_s = held([P, k_passes * T], U8, "tab_s")
-        w2_s_raw = held([P, k_passes, H], U8, "w2_s_raw")
+        w2_s_raw = held([P, k_passes, H], U8, "w2_s_raw", offset=0)
         tab_s_words = tab_s[:].bitcast(I32)
         nc.vector.memset(tab_s_words[:, : T // 4], 0)
         nc.gpsimd.memset(tab_s_words[:, T // 4 :], 0)
         w2_s_words = w2_s_raw[:].rearrange("p a c -> p (a c)").bitcast(I32)
         nc.vector.memset(w2_s_words[:, : H // 4], 0)
         nc.gpsimd.memset(w2_s_words[:, H // 4 :], 0)
-
-        nc.sync.dma_start(offs_t[:], offs)
-        nc.sync.dma_start(pos1_t[:], pos1)
-        nc.sync.dma_start(pos2_t[:], pos2)
-        rows = {}
-        for name, vec in (("scl", scl), ("expo", expo), ("base", base)):
-            rows[name] = held([P, r_passes * PACK], F32, name + "_t")
-            nc.sync.dma_start(
-                out=rows[name][:].rearrange("p (b i) -> p b i", i=PACK),
-                in_=vec.rearrange("(b p i) -> p b i", p=P, i=PACK),
-            )
 
         tab_w = [held([P, T], I32, f"tab_w{a}") for a in range(k_passes)]
         w2_w_raw = held([P, k_passes, H], U16, "w2_w_raw")
@@ -76,32 +69,44 @@ def tile_list_colony_confirmation_scores_kernel(
         def load_table(a):
             nc.sync.dma_start(out=tab_w[a][:], in_=tab_words[a].rearrange("p t i -> p (t i)").bitcast(I32))
 
-        def load_w1(b):
-            for a in range(k_passes):
-                nc.sync.dma_start(
-                    out=w1_raw[b, a][:],
-                    in_=w1[PASS * a : PASS * (a + 1), PASS * b : PASS * (b + 1)].rearrange("(p j) c -> p j c", j=PACK),
-                )
+        def load_w1(b, a):
+            nc.sync.dma_start(
+                out=w1_raw[b, a][:],
+                in_=w1[PASS * a : PASS * (a + 1), PASS * b : PASS * (b + 1)].rearrange("(p j) c -> p j c", j=PACK),
+            )
 
         def load_rows(tile, src, b):
             nc.sync.dma_start(out=tile[:], in_=src[PASS * b : PASS * (b + 1), :].rearrange("(p i) c -> p i c", i=PACK))
 
+        nc.sync.dma_start(offs_t[:], offs)
         load_table(0)
-        nc.sync.dma_start(out=w2_w_raw[:].bitcast(I32), in_=w2_words.rearrange("a p c -> p a c").bitcast(I32))
+        nc.sync.dma_start(pos1_t[:], pos1)
+        nc.sync.dma_start(pos2_t[:], pos2)
+        rows = {}
+        for name, vec in (("scl", scl), ("expo", expo), ("base", base)):
+            rows[name] = held([P, r_passes * PACK], F32, name + "_t")
+            nc.sync.dma_start(
+                out=rows[name][:].rearrange("p (b i) -> p b i", i=PACK),
+                in_=vec.rearrange("(b p i) -> p b i", p=P, i=PACK),
+            )
+
+        load_table(1)
         for q in range(4):
             nc.sync.dma_start(
                 out=tab_s_words[32 * q : 32 * q + 4, :].rearrange("r (a c) -> r a c", a=k_passes),
                 in_=tab_scales[:, 4 * q : 4 * q + 4, :].rearrange("a r c -> r a c").bitcast(I32),
             )
-        load_table(1)
+        nc.sync.dma_start(out=w2_w_raw[:].bitcast(I32), in_=w2_words.rearrange("a p c -> p a c").bitcast(I32))
         for q in range(4):
             nc.sync.dma_start(
                 out=w2_s_raw[32 * q : 32 * q + 4, :, :].bitcast(I32),
                 in_=w2_scales[:, 4 * q : 4 * q + 4, :].rearrange("a r c -> r a c").bitcast(I32),
             )
-        load_w1(0)
+        load_w1(0, 0)
+        load_w1(0, 1)
+        load_w1(1, 0)
+        load_w1(1, 1)
         load_rows(morph_t[0], morph, 0)
-        load_w1(1)
         load_rows(morph_t[1], morph, 1)
         load_rows(w3_raw[0], w3, 0)
         load_rows(w3_raw[1], w3, 1)
@@ -111,12 +116,14 @@ def tile_list_colony_confirmation_scores_kernel(
         def list_half(hf):
             return offs_t[:, hf * BANK // 16 : (hf + 1) * BANK // 16]
 
-        def gather_scales(a, hf):
-            v_s[a, hf] = held([P, BANK], U8, f"v_s{a}{hf}")
-            nc.vector.tensor_copy(out=v_s[a, hf][:], in_=tab_s[:, a * T : (a + 1) * T].indirect(list_half(hf)))
+        def gather_scales(hf, offset=None):
+            both = held([P, k_passes * BANK], U8, f"v_s{hf}", offset)
+            for a in range(k_passes):
+                v_s[a, hf] = both[:, a * BANK : (a + 1) * BANK]
+                nc.vector.tensor_copy(out=v_s[a, hf], in_=tab_s[:, a * T : (a + 1) * T].indirect(list_half(hf)))
 
-        def gather_words(a, hf):
-            v_w[a, hf] = held([P, BANK], U32, f"v_w{a}{hf}")
+        def gather_words(a, hf, offset=None):
+            v_w[a, hf] = held([P, BANK], U32, f"v_w{a}{hf}", offset)
             nc.vector.tensor_copy(out=v_w[a, hf][:], in_=tab_w[a][:].bitcast(U32).indirect(list_half(hf)))
 
         def deal_w2(raw, dtype, name):
@@ -128,14 +135,13 @@ def tile_list_colony_confirmation_scores_kernel(
             return dealt
 
         gather_words(0, 0)
-        w2_w = deal_w2(w2_w_raw, U16, "w2_w")
-        gather_scales(0, 0)
-        gather_scales(1, 0)
         gather_words(1, 0)
+        gather_scales(0)
+        w2_w = deal_w2(w2_w_raw, U16, "w2_w")
         w2_s = deal_w2(w2_s_raw, U8, "w2_s")
-        for a in range(k_passes):
-            gather_words(a, 1)
-            gather_scales(a, 1)
+        gather_words(0, 1)
+        gather_words(1, 1, k_passes * BANK)
+        gather_scales(1, 0)
 
         def quantise(grouped, name):
             codes = held([P, PASS], U32, name + "_c")
@@ -160,7 +166,10 @@ def tile_list_colony_confirmation_scores_kernel(
 
         def prepare_w3(b):
             grouped = rounded()
-            round_on_gpsimd(grouped[:].rearrange("p (n i) -> p n i", i=PACK), w3_raw[b][:].rearrange("p i n -> p n i"))
+            nc.vector.tensor_copy(
+                out=grouped[:].rearrange("p (c e i) -> p c i e", e=4, i=PACK),
+                in_=w3_raw[b][:].rearrange("p i (c e) -> p c i e", e=4),
+            )
             w3_q[b] = quantise(grouped, f"w3_q{b}")
 
         def first_stage(dst, hf, lhs_of_pass, copy_out):
@@ -172,7 +181,7 @@ def tile_list_colony_confirmation_scores_kernel(
                     lhsT=codes,
                     lhsT_scale=scales,
                     rhs=v_w[a, hf][:].bitcast(FP8X4),
-                    rhs_scale=v_s[a, hf][:],
+                    rhs_scale=v_s[a, hf],
                     start=(a == 0),
                     stop=(a == k_passes - 1),
                 )
@@ -256,65 +265,68 @@ def tile_list_colony_confirmation_scores_kernel(
                 out=x_f32[b][:, i, :], in0=g_t[b, i][:].indirect(pos2_t[:]), in1=share[b, i][:], op=ALU.add
             )
 
-        HALF = M // 2
-        y = {(hm, pair): fin.tile([P, 2, HALF], F32, name=f"y{hm}{pair}") for hm in range(2) for pair in range(2)}
+        n_tiles = N // P
+        parts = M // PART
+        y = [fin.tile([P, n_tiles, PART], F32, name=f"y{part}") for part in range(parts)]
 
-        def quantise_x(b, m0, width):
-            grouped = rounded()
+        def round_x(b, m0, width):
+            grouped = rounded()[:, : width * PACK]
             nc.vector.tensor_copy(
-                out=grouped[:, : width * PACK].rearrange("p (c e i) -> p c i e", e=4, i=PACK),
+                out=grouped.rearrange("p (c e i) -> p c i e", e=4, i=PACK),
                 in_=x_f32[b][:, :, m0 : m0 + width].rearrange("p i (c e) -> p c i e", e=4),
             )
-            codes = held([P, width], U32, f"x_c{b}{m0}")
-            scales = held([P, width], U8, f"x_s{b}{m0}")
-            nc.vector.quantize_mx(out=codes[:].bitcast(FP8X4), scales=scales[:], in_=grouped[:, : width * PACK])
+            return grouped
+
+        def quantise_x(grouped, width, name):
+            codes = held([P, width], U32, name + "_c")
+            scales = held([P, width], U8, name + "_s")
+            nc.vector.quantize_mx(out=codes[:].bitcast(FP8X4), scales=scales[:], in_=grouped)
             return codes, scales
 
-        def second_stage(b, hm, x_c, x_s):
+        def second_stage(b, part, x_c, x_s):
             w_c, w_s = w3_q[b]
-            for pair in range(2):
-                for u in range(2):
-                    cols = slice(P * (2 * pair + u), P * (2 * pair + u + 1))
-                    nc.tensor.matmul_mx(
-                        out=y[hm, pair][:, u, :],
-                        lhsT=w_c[:, cols].bitcast(FP8X4),
-                        lhsT_scale=w_s[:, cols],
-                        rhs=x_c.bitcast(FP8X4),
-                        rhs_scale=x_s,
-                        start=(b == 0 and u == 0),
-                        stop=(b == r_passes - 1 and u == 1),
-                    )
-
-        def finish(hm):
-            for pair in range(2):
-                res = held([P, 2, HALF], F32, f"res{hm}{pair}")
-                nc.scalar.activation(out=res[:], in_=y[hm, pair][:], func=ACT.Tanh)
-                nc.sync.dma_start(
-                    out=out[2 * P * pair : 2 * P * (pair + 1), hm * HALF : (hm + 1) * HALF].rearrange("(u p) m -> p u m", p=P),
-                    in_=res[:],
+            for nt in range(n_tiles):
+                cols = slice(P * nt, P * (nt + 1))
+                nc.tensor.matmul_mx(
+                    out=y[part][:, nt, :],
+                    lhsT=w_c[:, cols].bitcast(FP8X4),
+                    lhsT_scale=w_s[:, cols],
+                    rhs=x_c.bitcast(FP8X4),
+                    rhs_scale=x_s,
+                    start=(b == 0 and nt == 0),
+                    stop=(b == r_passes - 1 and nt == n_tiles - 1),
                 )
+
+        def finish(part):
+            res = held([P, n_tiles, PART], F32, f"res{part}")
+            nc.scalar.activation(out=res[:], in_=y[part][:], func=ACT.Tanh)
+            nc.sync.dma_start(
+                out=out[:, part * PART : (part + 1) * PART].rearrange("(u p) m -> p u m", p=P), in_=res[:]
+            )
 
         tiles = [(b, i) for b in range(r_passes) for i in range(PACK)]
         last = tiles[-1]
         for b, i in tiles:
             make_g(b, i, 0, nc.scalar.copy)
         prepare_w1(0)
-        for i in range(PACK):
-            make_g(0, i, 1, nc.scalar.copy)
-        for i in range(PACK):
-            make_g(1, i, 1, nc.vector.tensor_copy)
+        look(*tiles[0])
+        for b, i in tiles[:PACK] + [last]:
+            make_g(b, i, 1, nc.vector.tensor_copy)
         picked_last = held([P, M], F32, "picked_last")
         nc.vector.tensor_copy(out=picked_last[:], in_=g_t[last][:].indirect(pos2_t[:]))
         for n, tile in enumerate(tiles):
             before = tiles[n - 1] if n > 0 else None
             if n == 2:
                 prepare_w1(1)
-            if n == 5:
+            if n == 4:
                 prepare_w3(0)
-            if n == 7:
+            if n == 6:
                 prepare_w3(1)
-            look(*tile)
-            if n < SUMS_ON_SCALAR:
+            if before:
+                look(*tile)
+            if 1 <= n < PACK:
+                make_g(1, n - 1, 1, nc.scalar.copy)
+            if n >= SUMS_ON_VECTOR:
                 row_sum_on_scalar(*tile)
             else:
                 row_sum(*tile)
@@ -323,17 +335,18 @@ def tile_list_colony_confirmation_scores_kernel(
             invert(*tile)
             if before:
                 add_picked(*before)
-            if n == 6:
-                x_c, x_s = quantise_x(0, 0, M)
-                for hm in range(2):
-                    cols = slice(hm * HALF, (hm + 1) * HALF)
-                    second_stage(0, hm, x_c[:, cols], x_s[:, cols])
+            if n == 5:
+                x_c, x_s = quantise_x(round_x(0, 0, M), M, "x_q0")
+                for part in range(parts):
+                    cols = slice(part * PART, (part + 1) * PART)
+                    second_stage(0, part, x_c[:, cols], x_s[:, cols])
 
         b, i = last
         weighed_last = held([P, M], F32, "weighed_last")
         nc.vector.tensor_tensor(out=weighed_last[:], in0=a_t[last][:], in1=morph_t[b][:, i, :], op=ALU.mult)
-        for hm in range(2):
-            cols = slice(hm * HALF, (hm + 1) * HALF)
+
+        def join_last(part):
+            cols = slice(part * PART, (part + 1) * PART)
             nc.vector.scalar_tensor_tensor(
                 out=x_f32[b][:, i, cols],
                 in0=weighed_last[:, cols],
@@ -342,7 +355,14 @@ def tile_list_colony_confirmation_scores_kernel(
                 op0=ALU.mult,
                 op1=ALU.add,
             )
-        for hm in range(2):
-            x_c, x_s = quantise_x(b, hm * HALF, HALF)
-            second_stage(b, hm, x_c[:], x_s[:])
-            finish(hm)
+
+        grouped = {}
+        for step in range(parts + 2):
+            if step < parts:
+                join_last(step)
+            if 1 <= step <= parts:
+                grouped[step - 1] = round_x(b, (step - 1) * PART, PART)
+            if step >= 2:
+                x_c, x_s = quantise_x(grouped[step - 2], PART, f"x_q1{step}")
+                second_stage(b, step - 2, x_c[:], x_s[:])
+                finish(step - 2)

@@ -47,6 +47,9 @@ def tile_list_colony_confirmation_scores_kernel(
         def rounded():
             return keep.tile([P, PASS * PACK], BF16, name="rounded", bufs=4, align_bytes=64)
 
+        def rounded_in_turn(name):
+            return keep.tile([P, PASS * PACK], BF16, name=name, tag="in_turn", align_bytes=64)
+
         offs_t = held([P, S // 16], U16, "offs_t")
         pos1_t = held([P, M // 16], U16, "pos1_t")
         pos2_t = held([P, M // 16], U16, "pos2_t")
@@ -104,12 +107,11 @@ def tile_list_colony_confirmation_scores_kernel(
             )
         load_w1(0, 0)
         load_w1(0, 1)
-        load_w1(1, 0)
-        load_w1(1, 1)
+        for n in range(2):
+            load_rows(w3_raw[n], w3, n)
+            load_w1(1, n)
         load_rows(morph_t[0], morph, 0)
         load_rows(morph_t[1], morph, 1)
-        load_rows(w3_raw[0], w3, 0)
-        load_rows(w3_raw[1], w3, 1)
 
         v_s, v_w = {}, {}
 
@@ -156,7 +158,7 @@ def tile_list_colony_confirmation_scores_kernel(
 
         def prepare_w1(b):
             for a in range(k_passes):
-                grouped = rounded()
+                grouped = rounded_in_turn("w1_last") if (b, a) == (0, k_passes - 1) else rounded()
                 dst = grouped[:].rearrange("p (t m j) -> p m t j", t=PACK, j=PACK)
                 src = w1_raw[b, a][:].rearrange("p j (m t) -> p m t j", t=PACK)
                 round_on_gpsimd(dst, src)
@@ -165,14 +167,14 @@ def tile_list_colony_confirmation_scores_kernel(
         w3_q = {}
 
         def prepare_w3(b):
-            grouped = rounded()
+            grouped = rounded_in_turn(f"w3_g{b}")
             nc.vector.tensor_copy(
                 out=grouped[:].rearrange("p (c e i) -> p c i e", e=4, i=PACK),
                 in_=w3_raw[b][:].rearrange("p i (c e) -> p c i e", e=4),
             )
             w3_q[b] = quantise(grouped, f"w3_q{b}")
 
-        def first_stage(dst, hf, lhs_of_pass, copy_out):
+        def first_stage(dst, hf, lhs_of_pass):
             bank = acc.tile([P, BANK], F32, name="bank")
             for a in range(k_passes):
                 codes, scales = lhs_of_pass(a)
@@ -185,18 +187,18 @@ def tile_list_colony_confirmation_scores_kernel(
                     start=(a == 0),
                     stop=(a == k_passes - 1),
                 )
-            copy_out(out=dst[:, hf * BANK : (hf + 1) * BANK], in_=bank[:])
+            nc.scalar.copy(out=dst[:, hf * BANK : (hf + 1) * BANK], in_=bank[:])
 
         g_t = {(b, i): held([P, S], F32, f"g{b}{i}") for b in range(r_passes) for i in range(PACK)}
 
-        def make_g(b, i, hf, copy_out):
+        def make_g(b, i, hf):
             c0 = PASS * b + P * i
 
             def lhs(a):
                 cols = slice(a * H + c0, a * H + c0 + P)
                 return w2_w[:, cols].bitcast(FP4X4), w2_s[:, cols]
 
-            first_stage(g_t[b, i], hf, lhs, copy_out)
+            first_stage(g_t[b, i], hf, lhs)
 
         denom = held([P, r_passes * PACK], F32, "denom")
         inv = held([P, r_passes * PACK], F32, "inv")
@@ -205,6 +207,16 @@ def tile_list_colony_confirmation_scores_kernel(
 
         def col(b, i):
             return slice(PACK * b + i, PACK * b + i + 1)
+
+        tiles = [(b, i) for b in range(r_passes) for i in range(PACK)]
+        last = tiles[-1]
+
+        def denominator(b, i):
+            n = tiles.index((b, i))
+            if (b, i) in (tiles[0], last):
+                return denom[:, col(b, i)]
+            b0, i0 = tiles[n - 1]
+            return x_f32[b0][:, i0, 0:1]
 
         def look(b, i):
             h_t = ring.tile([P, S], F32, name="h_t")
@@ -215,7 +227,7 @@ def tile_list_colony_confirmation_scores_kernel(
                 return codes[:, cols].bitcast(FP8X4), scales[:, cols]
 
             for hf in range(halves):
-                first_stage(h_t, hf, lhs, nc.scalar.copy)
+                first_stage(h_t, hf, lhs)
             a_t[b, i] = ring.tile([P, M], F32, name="a_t")
             nc.scalar.activation(
                 out=a_t[b, i][:],
@@ -231,7 +243,7 @@ def tile_list_colony_confirmation_scores_kernel(
             passed = ring.tile([P, M], BF16, name="passed_s")
             nc.scalar.activation(out=passed[:], in_=a_t[b, i][:], func=ACT.Copy, accum_out=sums[:, col(b, i)])
             nc.scalar.activation(
-                out=denom[:, col(b, i)], in_=sums[:, col(b, i)], func=ACT.Identity, bias=rows["base"][:, col(b, i)]
+                out=denominator(b, i), in_=sums[:, col(b, i)], func=ACT.Identity, bias=rows["base"][:, col(b, i)]
             )
 
         def row_sum(b, i):
@@ -243,11 +255,11 @@ def tile_list_colony_confirmation_scores_kernel(
                 scalar2=rows["base"][:, col(b, i)],
                 op0=ALU.mult,
                 op1=ALU.add,
-                accum_out=denom[:, col(b, i)],
+                accum_out=denominator(b, i),
             )
 
         def invert(b, i):
-            nc.vector.reciprocal(out=inv[:, col(b, i)], in_=denom[:, col(b, i)])
+            nc.vector.reciprocal(out=inv[:, col(b, i)], in_=denominator(b, i))
 
         def weigh(b, i):
             share[b, i] = ring.tile([P, M], F32, name="share")
@@ -304,28 +316,22 @@ def tile_list_colony_confirmation_scores_kernel(
                 out=out[:, part * PART : (part + 1) * PART].rearrange("(u p) m -> p u m", p=P), in_=res[:]
             )
 
-        tiles = [(b, i) for b in range(r_passes) for i in range(PACK)]
-        last = tiles[-1]
         for b, i in tiles:
-            make_g(b, i, 0, nc.scalar.copy)
+            make_g(b, i, 0)
         prepare_w1(0)
-        look(*tiles[0])
-        for b, i in tiles[:PACK] + [last]:
-            make_g(b, i, 1, nc.vector.tensor_copy)
+        for b in range(r_passes):
+            prepare_w3(b)
         picked_last = held([P, M], F32, "picked_last")
-        nc.vector.tensor_copy(out=picked_last[:], in_=g_t[last][:].indirect(pos2_t[:]))
         for n, tile in enumerate(tiles):
             before = tiles[n - 1] if n > 0 else None
             if n == 2:
                 prepare_w1(1)
-            if n == 4:
-                prepare_w3(0)
-            if n == 6:
-                prepare_w3(1)
-            if before:
-                look(*tile)
-            if 1 <= n < PACK:
-                make_g(1, n - 1, 1, nc.scalar.copy)
+            look(*tile)
+            if tile != last:
+                make_g(*tile, 1)
+            if n == 5:
+                make_g(*last, 1)
+                nc.vector.tensor_copy(out=picked_last[:], in_=g_t[last][:].indirect(pos2_t[:]))
             if n >= SUMS_ON_VECTOR:
                 row_sum_on_scalar(*tile)
             else:

from contextlib import ExitStack

import concourse.mybir as mybir

K, H, N, T, S, M = 1024, 1024, 512, 2048, 1024, 512
FLOPS = 2 * (2 * K * H * S + H * N * M)

F32 = mybir.dt.float32
BF16 = mybir.dt.bfloat16
I32 = mybir.dt.int32
U32 = mybir.dt.uint32
U16 = mybir.dt.uint16
U8 = mybir.dt.uint8
FP8X4 = mybir.dt.float8_e4m3fn_x4
FP4X4 = mybir.dt.float4_e2m1fn_x4
ACT = mybir.ActivationFunctionType
ALU = mybir.AluOpType

P = 128
PACK = 4
PASS = P * PACK
BANK = 512
PART = 128
SUMS_ON_VECTOR = 3


def tile_list_colony_confirmation_scores_kernel(
    tc, tab_words, tab_scales, offs, pos1, pos2, w1, w2_words, w2_scales, scl, expo, base, morph, w3, out
):
    nc = tc.nc
    k_passes = K // PASS
    r_passes = H // PASS
    halves = S // BANK

    with ExitStack() as ctx:
        keep = ctx.enter_context(tc.tile_pool(name="keep", bufs=1))
        shared = ctx.enter_context(tc.tile_pool(name="shared", bufs=1))
        ring = ctx.enter_context(tc.tile_pool(name="ring", bufs=3))
        acc = ctx.enter_context(tc.psum_pool(name="acc", bufs=4))
        fin = ctx.enter_context(tc.psum_pool(name="fin", bufs=1))

        def held(shape, dtype, name, offset=None):
            if offset is None:
                return keep.tile(shape, dtype, name=name, align_bytes=64)
            return shared.tile(shape, dtype, name=name, align_bytes=64, offset=offset)

        def rounded():
            return keep.tile([P, PASS * PACK], BF16, name="rounded", bufs=4, align_bytes=64)

        def rounded_in_turn(name):
            return keep.tile([P, PASS * PACK], BF16, name=name, tag="in_turn", align_bytes=64)

        offs_t = held([P, S // 16], U16, "offs_t")
        pos1_t = held([P, M // 16], U16, "pos1_t")
        pos2_t = held([P, M // 16], U16, "pos2_t")

        tab_s = held([P, k_passes * T], U8, "tab_s")
        w2_s_raw = held([P, k_passes, H], U8, "w2_s_raw", offset=0)
        tab_s_words = tab_s[:].bitcast(I32)
        nc.vector.memset(tab_s_words[:, : T // 4], 0)
        nc.gpsimd.memset(tab_s_words[:, T // 4 :], 0)
        w2_s_words = w2_s_raw[:].rearrange("p a c -> p (a c)").bitcast(I32)
        nc.vector.memset(w2_s_words[:, : H // 4], 0)
        nc.gpsimd.memset(w2_s_words[:, H // 4 :], 0)

        tab_w = [held([P, T], I32, f"tab_w{a}") for a in range(k_passes)]
        w2_w_raw = held([P, k_passes, H], U16, "w2_w_raw")
        w1_raw = {(b, a): held([P, PACK, PASS], F32, f"w1_raw{b}{a}") for b in range(r_passes) for a in range(k_passes)}
        morph_t = [held([P, PACK, M], F32, f"morph_t{b}") for b in range(r_passes)]
        w3_raw = [held([P, PACK, N], F32, f"w3_raw{b}") for b in range(r_passes)]

        def load_table(a):
            nc.sync.dma_start(out=tab_w[a][:], in_=tab_words[a].rearrange("p t i -> p (t i)").bitcast(I32))

        def load_w1(b, a):
            nc.sync.dma_start(
                out=w1_raw[b, a][:],
                in_=w1[PASS * a : PASS * (a + 1), PASS * b : PASS * (b + 1)].rearrange("(p j) c -> p j c", j=PACK),
            )

        def load_rows(tile, src, b):
            nc.sync.dma_start(out=tile[:], in_=src[PASS * b : PASS * (b + 1), :].rearrange("(p i) c -> p i c", i=PACK))

        nc.sync.dma_start(offs_t[:], offs)
        load_table(0)
        nc.sync.dma_start(pos1_t[:], pos1)
        nc.sync.dma_start(pos2_t[:], pos2)
        rows = {}
        for name, vec in (("scl", scl), ("expo", expo), ("base", base)):
            rows[name] = held([P, r_passes * PACK], F32, name + "_t")
            nc.sync.dma_start(
                out=rows[name][:].rearrange("p (b i) -> p b i", i=PACK),
                in_=vec.rearrange("(b p i) -> p b i", p=P, i=PACK),
            )

        load_table(1)
        for q in range(4):
            nc.sync.dma_start(
                out=tab_s_words[32 * q : 32 * q + 4, :].rearrange("r (a c) -> r a c", a=k_passes),
                in_=tab_scales[:, 4 * q : 4 * q + 4, :].rearrange("a r c -> r a c").bitcast(I32),
            )
        nc.sync.dma_start(out=w2_w_raw[:].bitcast(I32), in_=w2_words.rearrange("a p c -> p a c").bitcast(I32))
        for q in range(4):
            nc.sync.dma_start(
                out=w2_s_raw[32 * q : 32 * q + 4, :, :].bitcast(I32),
                in_=w2_scales[:, 4 * q : 4 * q + 4, :].rearrange("a r c -> r a c").bitcast(I32),
            )
        load_w1(0, 0)
        load_w1(0, 1)
        for n in range(2):
            load_rows(w3_raw[n], w3, n)
            load_w1(1, n)
        load_rows(morph_t[0], morph, 0)
        load_rows(morph_t[1], morph, 1)

        v_s, v_w = {}, {}

        def list_half(hf):
            return offs_t[:, hf * BANK // 16 : (hf + 1) * BANK // 16]

        def gather_scales(hf, offset=None):
            both = held([P, k_passes * BANK], U8, f"v_s{hf}", offset)
            for a in range(k_passes):
                v_s[a, hf] = both[:, a * BANK : (a + 1) * BANK]
                nc.vector.tensor_copy(out=v_s[a, hf], in_=tab_s[:, a * T : (a + 1) * T].indirect(list_half(hf)))

        def gather_words(a, hf, offset=None):
            v_w[a, hf] = held([P, BANK], U32, f"v_w{a}{hf}", offset)
            nc.vector.tensor_copy(out=v_w[a, hf][:], in_=tab_w[a][:].bitcast(U32).indirect(list_half(hf)))

        def deal_w2(raw, dtype, name):
            dealt = held([P, k_passes * H], dtype, name)
            nc.vector.tensor_copy(
                out=dealt[:].rearrange("p (g t m) -> p g t m", t=PACK, m=P),
                in_=raw[:].rearrange("p a (b m t) -> p (a b) t m", t=PACK, m=P),
            )
            return dealt

        gather_words(0, 0)
        gather_words(1, 0)
        gather_scales(0)
        w2_w = deal_w2(w2_w_raw, U16, "w2_w")
        w2_s = deal_w2(w2_s_raw, U8, "w2_s")
        gather_words(0, 1)
        gather_words(1, 1, k_passes * BANK)
        gather_scales(1, 0)

        def quantise(grouped, name):
            codes = held([P, PASS], U32, name + "_c")
            scales = held([P, PASS], U8, name + "_s")
            nc.vector.quantize_mx(out=codes[:].bitcast(FP8X4), scales=scales[:], in_=grouped[:])
            return codes, scales

        def round_on_gpsimd(dst, src):
            nc.gpsimd.tensor_scalar(out=dst, in0=src, scalar1=1.0, scalar2=0.0, op0=ALU.mult, op1=ALU.add)

        w1_q = {}

        def prepare_w1(b):
            for a in range(k_passes):
                grouped = rounded_in_turn("w1_last") if (b, a) == (0, k_passes - 1) else rounded()
                dst = grouped[:].rearrange("p (t m j) -> p m t j", t=PACK, j=PACK)
                src = w1_raw[b, a][:].rearrange("p j (m t) -> p m t j", t=PACK)
                round_on_gpsimd(dst, src)
                w1_q[b, a] = quantise(grouped, f"w1_q{b}{a}")

        w3_q = {}

        def prepare_w3(b):
            grouped = rounded_in_turn(f"w3_g{b}")
            nc.vector.tensor_copy(
                out=grouped[:].rearrange("p (c e i) -> p c i e", e=4, i=PACK),
                in_=w3_raw[b][:].rearrange("p i (c e) -> p c i e", e=4),
            )
            w3_q[b] = quantise(grouped, f"w3_q{b}")

        def first_stage(dst, hf, lhs_of_pass):
            bank = acc.tile([P, BANK], F32, name="bank")
            for a in range(k_passes):
                codes, scales = lhs_of_pass(a)
                nc.tensor.matmul_mx(
                    out=bank[:],
                    lhsT=codes,
                    lhsT_scale=scales,
                    rhs=v_w[a, hf][:].bitcast(FP8X4),
                    rhs_scale=v_s[a, hf],
                    start=(a == 0),
                    stop=(a == k_passes - 1),
                )
            nc.scalar.copy(out=dst[:, hf * BANK : (hf + 1) * BANK], in_=bank[:])

        g_t = {(b, i): held([P, S], F32, f"g{b}{i}") for b in range(r_passes) for i in range(PACK)}

        def make_g(b, i, hf):
            c0 = PASS * b + P * i

            def lhs(a):
                cols = slice(a * H + c0, a * H + c0 + P)
                return w2_w[:, cols].bitcast(FP4X4), w2_s[:, cols]

            first_stage(g_t[b, i], hf, lhs)

        denom = held([P, r_passes * PACK], F32, "denom")
        inv = held([P, r_passes * PACK], F32, "inv")
        x_f32 = [held([P, PACK, M], F32, f"x_f32{b}") for b in range(r_passes)]
        a_t, share = {}, {}

        def col(b, i):
            return slice(PACK * b + i, PACK * b + i + 1)

        tiles = [(b, i) for b in range(r_passes) for i in range(PACK)]
        last = tiles[-1]

        def denominator(b, i):
            n = tiles.index((b, i))
            if (b, i) in (tiles[0], last):
                return denom[:, col(b, i)]
            b0, i0 = tiles[n - 1]
            return x_f32[b0][:, i0, 0:1]

        def look(b, i):
            h_t = ring.tile([P, S], F32, name="h_t")

            def lhs(a):
                codes, scales = w1_q[b, a]
                cols = slice(P * i, P * (i + 1))
                return codes[:, cols].bitcast(FP8X4), scales[:, cols]

            for hf in range(halves):
                first_stage(h_t, hf, lhs)
            a_t[b, i] = ring.tile([P, M], F32, name="a_t")
            nc.scalar.activation(
                out=a_t[b, i][:],
                in_=h_t[:].indirect(pos1_t[:]),
                func=ACT.Exp,
                bias=rows["expo"][:, col(b, i)],
                scale=rows["scl"][:, col(b, i)],
            )

        sums = held([P, r_passes * PACK], F32, "sums")

        def row_sum_on_scalar(b, i):
            passed = ring.tile([P, M], BF16, name="passed_s")
            nc.scalar.activation(out=passed[:], in_=a_t[b, i][:], func=ACT.Copy, accum_out=sums[:, col(b, i)])
            nc.scalar.activation(
                out=denominator(b, i), in_=sums[:, col(b, i)], func=ACT.Identity, bias=rows["base"][:, col(b, i)]
            )

        def row_sum(b, i):
            passed = ring.tile([P, M], BF16, name="passed")
            nc.vector.tensor_scalar(
                out=passed[:],
                in0=a_t[b, i][:],
                scalar1=1.0,
                scalar2=rows["base"][:, col(b, i)],
                op0=ALU.mult,
                op1=ALU.add,
                accum_out=denominator(b, i),
            )

        def invert(b, i):
            nc.vector.reciprocal(out=inv[:, col(b, i)], in_=denominator(b, i))

        def weigh(b, i):
            share[b, i] = ring.tile([P, M], F32, name="share")
            nc.vector.scalar_tensor_tensor(
                out=share[b, i][:],
                in0=a_t[b, i][:],
                scalar=inv[:, col(b, i)],
                in1=morph_t[b][:, i, :],
                op0=ALU.mult,
                op1=ALU.mult,
            )

        def add_picked(b, i):
            nc.vector.tensor_tensor(
                out=x_f32[b][:, i, :], in0=g_t[b, i][:].indirect(pos2_t[:]), in1=share[b, i][:], op=ALU.add
            )

        n_tiles = N // P
        parts = M // PART
        y = [fin.tile([P, n_tiles, PART], F32, name=f"y{part}") for part in range(parts)]

        def round_x(b, m0, width):
            grouped = rounded()[:, : width * PACK]
            nc.vector.tensor_copy(
                out=grouped.rearrange("p (c e i) -> p c i e", e=4, i=PACK),
                in_=x_f32[b][:, :, m0 : m0 + width].rearrange("p i (c e) -> p c i e", e=4),
            )
            return grouped

        def quantise_x(grouped, width, name):
            codes = held([P, width], U32, name + "_c")
            scales = held([P, width], U8, name + "_s")
            nc.vector.quantize_mx(out=codes[:].bitcast(FP8X4), scales=scales[:], in_=grouped)
            return codes, scales

        def second_stage(b, part, x_c, x_s):
            w_c, w_s = w3_q[b]
            for nt in range(n_tiles):
                cols = slice(P * nt, P * (nt + 1))
                nc.tensor.matmul_mx(
                    out=y[part][:, nt, :],
                    lhsT=w_c[:, cols].bitcast(FP8X4),
                    lhsT_scale=w_s[:, cols],
                    rhs=x_c.bitcast(FP8X4),
                    rhs_scale=x_s,
                    start=(b == 0 and nt == 0),
                    stop=(b == r_passes - 1 and nt == n_tiles - 1),
                )

        def finish(part):
            res = held([P, n_tiles, PART], F32, f"res{part}")
            nc.scalar.activation(out=res[:], in_=y[part][:], func=ACT.Tanh)
            nc.sync.dma_start(
                out=out[:, part * PART : (part + 1) * PART].rearrange("(u p) m -> p u m", p=P), in_=res[:]
            )

        for b, i in tiles:
            make_g(b, i, 0)
        prepare_w1(0)
        for b in range(r_passes):
            prepare_w3(b)
        picked_last = held([P, M], F32, "picked_last")
        for n, tile in enumerate(tiles):
            before = tiles[n - 1] if n > 0 else None
            if n == 2:
                prepare_w1(1)
            look(*tile)
            if tile != last:
                make_g(*tile, 1)
            if n == 5:
                make_g(*last, 1)
                nc.vector.tensor_copy(out=picked_last[:], in_=g_t[last][:].indirect(pos2_t[:]))
            if n >= SUMS_ON_VECTOR:
                row_sum_on_scalar(*tile)
            else:
                row_sum(*tile)
            if before:
                weigh(*before)
            invert(*tile)
            if before:
                add_picked(*before)
            if n == 5:
                x_c, x_s = quantise_x(round_x(0, 0, M), M, "x_q0")
                for part in range(parts):
                    cols = slice(part * PART, (part + 1) * PART)
                    second_stage(0, part, x_c[:, cols], x_s[:, cols])

        b, i = last
        weighed_last = held([P, M], F32, "weighed_last")
        nc.vector.tensor_tensor(out=weighed_last[:], in0=a_t[last][:], in1=morph_t[b][:, i, :], op=ALU.mult)

        def join_last(part):
            cols = slice(part * PART, (part + 1) * PART)
            nc.vector.scalar_tensor_tensor(
                out=x_f32[b][:, i, cols],
                in0=weighed_last[:, cols],
                scalar=inv[:, col(b, i)],
                in1=picked_last[:, cols],
                op0=ALU.mult,
                op1=ALU.add,
            )

        grouped = {}
        for step in range(parts + 2):
            if step < parts:
                join_last(step)
            if 1 <= step <= parts:
                grouped[step - 1] = round_x(b, (step - 1) * PART, PART)
            if step >= 2:
                x_c, x_s = quantise_x(grouped[step - 2], PART, f"x_q1{step}")
                second_stage(b, step - 2, x_c[:], x_s[:])
                finish(step - 2)
